import numpy as np, ml_dtypes
CORES = [3,7,11,15,131,135,139,143]
N = 8
import mx_ref
BF = ml_dtypes.bfloat16
def gentries(a):
    return np.ascontiguousarray(a.reshape(8, 16, -1).transpose(0, 2, 1)).reshape(8, -1)
def gtable(e):
    e = np.asarray(e); return np.ascontiguousarray(e.reshape(8, -1, 16).transpose(0, 2, 1)).reshape(128, -1).astype(np.int32)
def gcols(t, e):
    v = np.concatenate([t.reshape(8, 16, -1, 4), np.zeros((8, 16, 1, 4), BF)], axis=2)
    return np.ascontiguousarray(np.stack([v[g][:, e[g]] for g in range(8)])).reshape(128, -1)
def tile(rs):
    return np.stack(rs, axis=2).reshape(128, -1).astype(BF)
def pick(q, e):
    c = np.concatenate([q[0].reshape(128, -1, 4), np.zeros((128, 1, 4), np.uint8)], axis=1); s = np.concatenate([q[1], np.ones((16, 1), np.uint8)], axis=1)
    return (np.ascontiguousarray(c[:, e].reshape(128, -1)), np.ascontiguousarray(s[:, e]))
def join(*qs):
    return (np.concatenate([q[0] for q in qs], axis=1), np.concatenate([q[1] for q in qs], axis=1))
def put(q, e, v):
    c, s = q[0].reshape(128, -1, 4).copy(), q[1].copy(); c[:, e] = v[0].reshape(128, -1, 4); s[:, e] = v[1]
    return (c.reshape(128, -1), s)
def pk(c, s):
    return (np.ascontiguousarray(c), mx_ref.live(s))
def emit(q):
    return q[0], q[1]
def packed(v, rng):
    q = [mx_ref.quantize(np.ascontiguousarray(v[r])) for r in range(N)]
    return np.stack([a for a, b in q]), np.stack([mx_ref.plane(b, rng) for a, b in q])
def values_of_codes():
    e, c = np.zeros((128, 128, 4), np.float32), np.zeros((128, 2, 4), np.uint8)
    e[np.arange(128), np.arange(128), 0] = 1
    c[:127, :, 0] = np.arange(256).reshape(2, 128).T[:127]
    return mx_ref.matmul(mx_ref.quantize(e.reshape(128, 512).astype(BF)), (c.reshape(128, 8), np.full((16, 2), 127, np.uint8))).T.reshape(-1).astype(np.float64)
CODE_VALUE, SCALE_VALUE = values_of_codes(), 2.0 ** (np.arange(256) - 127.0)
def decode(q):
    return (CODE_VALUE[q[0]].reshape(16, 8, -1, 4) * SCALE_VALUE[q[1]][:, None, :, None] + 0.0).reshape(128, -1).astype(np.float32)
def f(rng, *shape):
    return mx_ref.flush((rng.standard_normal(shape, dtype=np.float32) * np.exp2(rng.integers(-2, 3, shape[:-1] + (1,)))).astype(BF))
def wide(rng, *shape, cols=0):
    v = rng.standard_normal(shape, dtype=np.float32) * np.exp2(rng.integers(-12, 13, shape)).astype(np.float32)
    if cols: v *= np.repeat(np.exp2(rng.integers(-cols, cols + 1, shape[:-2] + (1, shape[-1] // 4))) * (rng.random(shape[:-2] + (1, shape[-1] // 4)) > 0.0625), 4, axis=-1).astype(np.float32)
    return mx_ref.flush(v.astype(BF))
C, H, R = 256, 96, 3
def big(v):
    v = v.astype(np.float32)
    v[np.abs(v) < np.float32(2.0 ** -16)] = 0
    return v.astype(BF)
def numbers_of(rng):
    return {"x": big(f(rng, N, 128, 4 * C)), "u": np.array(f(rng, N, 128, 512)), "v": np.array(f(rng, N, 128, 512))}
def layers(rng, still=[]):
    w = big(f(rng, N, 128, 2048)).reshape(N, 8, 16, 4, 8, 16, 4)
    for i in still: w[:, :, :, :, :, i] = 0
    return w
def weights(rng, w):
    c, s = packed(np.ascontiguousarray(w).reshape(N, 128, 2048), rng)
    return {"wc": c, "ws": s}
def holes(rng):
    return np.sort(np.argsort(rng.random((N, 8, C - 1)), axis=2)[:, :, :H], axis=2)
def throws(rng, a):
    free = np.ones((N, 8, 2 * C), bool)
    free[:, :, C:] = False
    np.put_along_axis(free, a, False, axis=2)
    np.put_along_axis(free, C + np.roll(a, -1, axis=0), True, axis=2)
    e = np.zeros((N, 8, C), np.int64)
    for i in range(C - 1, -1, -1):
        k = (0.5 + rng.random((N, 8, C))) * free[:, :, i:i + C]
        k[:, :, C - 1] = 2.0 * free[:, :, i + C - 1]
        e[:, :, i] = i + np.argmax(k, axis=2)
        np.put_along_axis(free, e[:, :, i:i + 1], False, axis=2)
    return e
def lists(e):
    return np.stack([gtable(e[r]) for r in range(N)])
def meet(rng, e):
    used, out = [False] * C, []
    e = e.tolist()
    for i, k in zip(rng.permutation(C).tolist(), rng.integers(0, 4, C).tolist()):
        j = e[i] + (0, 1, 1 - C, -C)[k]
        if 0 <= j < C and j != i and not used[i] and not used[j]:
            used[i] = used[j] = True
            out += [i, j]
    return np.array(out + [int(i) for i in rng.permutation(C) if not used[i]])
def setup_inputs(rng):
    return {**numbers_of(rng), "p": lists(throws(rng, holes(rng))), **weights(rng, layers(rng))}
def setup_inputs_ties(rng):
    d = numbers_of(rng)
    o = rng.permutation(N)
    x = d["x"].reshape(N, 8, 16, C, 4)
    k = rng.integers(0, 3, (N, 8, C))
    k[o[2]] = 1
    x[:, :, 0] = 0
    x[:, :, 0, :, 0] = k.astype(np.float32).astype(BF)
    u = d["u"].reshape(N, 128, 128, 4)
    u[:, :, ::16] = 0
    for r in range(N):
        for h in range(0, 128, 16): u[r, h, h, 0] = 0.0 if r == o[0] else -1.0 if r == o[1] else 1.0
    return {"x": x.reshape(N, 128, 4 * C), "u": u.reshape(N, 128, 512), "v": d["v"], "p": lists(throws(rng, holes(rng))), **weights(rng, layers(rng, [0]))}
def setup_inputs_near(rng):
    d = numbers_of(rng)
    o = rng.permutation(N) % 4
    low = rng.permutation(8)[:4]
    x = d["x"].astype(np.float32).reshape(N, 8, 16, C, 4)
    u = d["u"].reshape(N, 128, 128, 4)
    x[:, :, 0] = 0
    x[:, :, 8:] = 0
    u[:, :, ::16] = 0
    for r in range(N):
        k = 1.0 if o[r] == 0 else 2.0 ** -30
        if o[r] < 3:
            s = rng.integers(0, 16, (8, C))
            x[r, :, 8] = ((s[:, :, None] >> np.arange(4)) & 1) * np.exp2(np.arange(4) - 23.0)
        else:
            x[r, :, 8, :, 0] = rng.integers(8, 16, (8, C)) * rng.choice([-1.0, 1.0], (8, C)) * 2.0 ** -27
            for g in low: x[r, g, 8:10, :, 0] = rng.integers(8, 15, (2, C)) * 2.0 ** -30
        if o[r] < 2:
            x[r, :, 0, :, 0] = rng.choice([-1.0, 1.0], (8, C))
            x[r, :, 11, :, 0] = 2.0 ** -10
        if o[r] == 2:
            for g in rng.permutation(8)[:4]: x[r, g, 0, rng.integers(C), 0] = 2.0 ** 29
        for h in range(0, 128, 16):
            u[r, h + 8, h] = k
            if o[r] < 2:
                u[r, h, h, 0] = k
                u[r, h + 11, h, 0] = k
            if o[r] == 2: u[r, h, h, 0] = 1.0
            if o[r] == 3 and h // 16 in low: u[r, h + 9, h] = -k
    still = [0, 8, 9, 10, 11, 12, 13, 14, 15]
    w = layers(rng, still)
    w[:, :, still] = 0
    return {"x": x.reshape(N, 128, 4 * C).astype(BF), "u": u.reshape(N, 128, 512), "v": d["v"], "p": lists(throws(rng, holes(rng))), **weights(rng, w)}
def setup_inputs_huge(rng):
    d = numbers_of(rng)
    h, o = rng.permutation(8), rng.permutation(N)
    c = rng.choice([-1.0, 1.0], (N, 1, 1, C, 1))
    c[o == 0] = 1.0
    x = (0.9 + 0.1 * rng.random((N, 8, 16, C, 4))) * 2.0 ** 30
    x[:, h[4:]] *= c
    a = (0.9 + 0.1 * rng.random((N, 8, 16, 8, 4))) * 2.0 ** 30
    for r in range(N):
        if o[r] == 0: a[r] *= -1.0
        elif o[r] % 2 == 1:
            a[r] *= -1.0
            a[r, h[4:]] = 0
        else: a[r, h[:4]] = 0
    u = d["u"].reshape(N, 128, 128, 4)
    u[:, :, ::16] = a.reshape(N, 128, 8, 4).astype(np.float32).astype(BF)
    w = np.zeros((N, 128, 4, 128, 4), np.float32)
    i = np.arange(128)
    for b in range(4): w[:, i, b, i, b] = -1
    return {"x": x.astype(np.float32).reshape(N, 128, 4 * C).astype(BF), "u": u.reshape(N, 128, 512), "v": d["v"], "p": lists(throws(rng, holes(rng))), **weights(rng, w.astype(BF))}
def setup_inputs_edges(rng):
    d = numbers_of(rng)
    h, a = rng.permutation(8), holes(rng)
    a[:, h[:2]] = np.arange(H)
    a[:, h[2:4]] = np.arange(C - 1 - H, C - 1)
    e = throws(rng, a)
    e[:, h[:2]] = np.arange(C) + H
    x = d["x"].reshape(N, 8, 16, C, 4)
    x[:, :, :3] = 0
    for r in range(N):
        for g in range(8):
            n = np.zeros(C, np.int64)
            n[meet(rng, e[r, g])] = np.arange(C - 1, -1, -1)
            for i in range(3): x[r, g, i, :, 0] = ((n >> (6 - 3 * i)) & 7).astype(np.float32).astype(BF)
    k = np.exp2(rng.integers(-2, 3, (N, 8, 1, C, 1)))
    b = (2 * rng.integers(0, 8, (N, 8, 8, C, 4)) + 1) * 2.0 ** -16 * k
    b[:, :, 0, :, 0] = 1.96875 * k[:, :, 0, :, 0]
    b *= rng.choice([-1.0, 1.0], b.shape)
    x[:, :, 8:] = b.astype(np.float32).astype(BF)
    u = d["u"].reshape(N, 128, 128, 4)
    u[:, :, ::16] = 0
    for g in range(0, 128, 16):
        for i in range(3): u[:, g + i, g, 0] = 2.0 ** (6 - 3 * i)
    return {"x": x.reshape(N, 128, 4 * C), "u": u.reshape(N, 128, 512), "v": d["v"], "p": lists(e), **weights(rng, layers(rng, [0, 1, 2, 8, 9, 10, 11, 12, 13, 14, 15]))}
def setup_inputs_spread(rng):
    d = setup_inputs(rng)
    d["x"] = big(wide(rng, N, 128, 4 * C, cols=6))
    return d
def check_inputs(d):
    b = []
    for k in ("x", "u", "v"):
        a = np.abs(d[k].astype(np.float32))
        if not (np.isfinite(a).all() and ((a == 0) | (a >= 2.0 ** -30) & (a <= 2.0 ** 30)).all()): b.append("a value of " + k)
    e = np.stack([gentries(d["p"][r]) for r in range(N)]).astype(np.int64)
    t, s = e - np.arange(C), np.sort(e, axis=2)
    if ((t < 0) | (t >= C)).any(): b.append("p: a landing out of its column's bounds")
    if (s[:, :, 1:] == s[:, :, :-1]).any(): b.append("p: equal landings")
    if (np.count_nonzero(e >= C, axis=2) != H).any(): b.append("p: the number of crossing landings")
    k = np.concatenate([s[:, :, :C - H], np.roll(s[:, :, C - H:], 1, axis=0) - C], axis=2)
    if (np.sort(k, axis=2) != np.arange(C)).any(): b.append("p: crossing landings aren't the next rank's holes")
    none, least, most = [emit(mx_ref.quantize(np.full((128, 16), k, np.float32).astype(BF)))[1][0, 0] for k in (0.0, 2.0 ** -30, 2.0 ** 30)]
    for r in range(N):
        if ((d["wc"][r] == 0x7F) | (d["wc"][r] == 0xFF)).any(): b.append("wc: a code that is no number")
        s = mx_ref.live(d["ws"][r])
        if ((s != none) & ((s < least) | (s > most))).any(): b.append("ws: a scale out of range")
    return b
def reference(x, u, v, p, wc, ws):
    qu = [mx_ref.quantize(u[r]) for r in range(N)]
    lay = [pk(wc[r], ws[r]) for r in range(N)]
    now = [x[r] for r in range(N)]
    land = np.stack([gentries(p[r]) for r in range(N)]).astype(np.int64)
    for t in range(R):
        for r in range(N):
            s = mx_ref.matmul(qu[r], mx_ref.quantize(now[r]))[::16] + np.float32(0.0)
            o = np.argsort(-s, axis=1, kind="stable")
            a, b = o[:, ::2], o[:, 1::2]
            la, lb = np.take_along_axis(land[r], a, axis=1), np.take_along_axis(land[r], b, axis=1)
            ok = (a <= lb) & (lb < a + C) & (b <= la) & (la < b + C)
            np.put_along_axis(land[r], a, np.where(ok, lb, la), axis=1)
            np.put_along_axis(land[r], b, np.where(ok, la, lb), axis=1)
        back, hits = np.argsort(land, axis=2), np.sort(land, axis=2)
        given = [mx_ref.quantize(gcols(now[r], back[r][:, C - H:])) for r in range(N)]
        new = []
        for r in range(N):
            both = np.concatenate([now[r], decode(given[r - 1]).astype(BF)], axis=1)
            e = np.zeros((8, C), np.int64)
            np.put_along_axis(e, hits[r][:, :C - H], back[r][:, :C - H], axis=1)
            np.put_along_axis(e, hits[r - 1][:, C - H:] - C, np.stack([C + np.arange(H)] * 8), axis=1)
            z = ((gcols(both, e).astype(np.float32) + now[r].astype(np.float32)) * np.float32(0.5)).astype(BF)
            q = mx_ref.quantize(z)
            new.append(tile([mx_ref.matmul(pick(lay[r], np.arange(128 * b, 128 * b + 128)), q) * np.float32(0.03125) + z[:, b::4].astype(np.float32) for b in range(4)]))
        now = new
    y, ol = np.zeros((N, 128, C), np.float32), np.zeros((N, 8, C), np.float32)
    oc, osc = np.zeros((N, 128, 4 * C), np.uint8), np.zeros((N, 16, C), np.uint8)
    for r in range(N):
        q = mx_ref.quantize(now[r])
        y[r] = mx_ref.matmul(mx_ref.quantize(v[r]), q)
        ol[r] = land[r]
        oc[r], osc[r] = emit(q)
    return {"y": y, "ol": ol, "oc": oc, "osc": osc}

@@ -1,0 +1,350 @@
+from concourse.mybir import dt, AluOpType, ActivationFunctionType
+
+OP = AluOpType
+COPY = ActivationFunctionType.Copy
+ROUNDS = 3
+BIG = 1e29
+LIFT = 4096.0
+OFF = 0.46875
+FIELD = sum(1 << b for b in (8, 9, 18, 19, 20))
+
+CTILES = [("a", 256, ["b", 15, 14, 13]), ("b", 192, [12, 11, 10, 9]), ("c", 128, [8, 7, 6, 5]), ("d", 128, [4, 3, 2, 1])]
+
+PACKS = {
+    "rows": (256, "float32", ["irow", "kwa", "kwb", "kw", "ex", "pw", "yy", "fy", "sx", "so", "vr0", "vr1", "vr2", "lr0", "lr1", "lr2", "lr3"]),
+    "flist": (16, "float32", ["r16", "q1", "q2", "r1", "ok", "y", "zl", "e1", "e2", "own", "neg"]),
+    "ilist": (16, "int32", ["m16", "mm", "ii", "ss", "c2", "tt", "c1", "rho", "par", "rx", "sig", "tso", "its", "lst1", "lst2", "lst3"]),
+    "ulist": (16, "uint16", ["perm", "rho16", "rx16", "l16", "sig16", "ts16"]),
+    "cols": (1, "float32", ["k1", "k16", "kap0", "kap"]),
+}
+PLACE = {name: (buf, i * w, w) for buf, (w, _, names) in PACKS.items() for i, name in enumerate(names)}
+
+
+def _scratch():
+    s = {}
+
+    def sb(d, n, *names):
+        for name in names:
+            s[name] = ("sbuf", [128, n], d)
+
+    def mx(n, *names):
+        for name in names:
+            sb("float8_e4m3fn_x4", n, "q" + name)
+            sb("uint8", n, "s" + name)
+    for buf, (w, d, names) in PACKS.items():
+        sb(d, w * len(names), buf)
+    for t in range(ROUNDS + 1):
+        sb("bfloat16", 1024, "x%d" % t)
+        mx(256, "x%d" % t)
+    for t in range(ROUNDS):
+        mx(256, "l%d" % t, "z%d" % t)
+        sb("int32", 16, "la%d" % t, "xs%d" % t)
+        sb("bfloat16", 1024, "z%d" % t)
+        sb("bfloat16", 512, "w%d" % t)
+        sb("float32", 16, "rs%d" % t)
+        sb("bfloat16", 2048, "h%d" % t)
+    sb("bfloat16", 1024, "zz", "ab", "xh")
+    mx(512, "w", "e")
+    mx(128, "u", "r", "v", "g")
+    for n, k, _ in CTILES:
+        sb("bfloat16", 4 * k, "c" + n)
+        mx(k, "c" + n)
+    sb("bfloat16", 520, "one", "ee")
+    sb("bfloat16", 512, "g1", "g2", "usb", "vsb")
+    sb("float32", 256, "ft16", "feqk", "fmsk", "fd0r", "fd0a", "fd1", "ffw", "ysb")
+    sb("int32", 256, "prow")
+    sb("int32", 16, "lst0")
+    sb("bfloat16", 256, "ibf", "d0b", "bsum")
+    sb("bfloat16", 1920, "junk")
+    sb("int32", 1, "ipcol", "ik")
+    sb("float32", 1, "fkcol")
+    sb("int32", 8, "upick")
+    sb("uint16", 8, "u16")
+    for n in ("ps", "pc", "pp0", "pp1", "pp2", "pp3"):
+        s[n] = ("psum", [128, 512], "float32")
+    return s
+
+
+SCRATCH = _scratch()
+SEMAPHORES = (["vec", "sca", "ten", "gps", "dx", "du", "dp", "dr", "dw", "dv", "dq", "dy", "dl", "loc"]
+              + ["ca%d" % t for t in range(ROUNDS)] + ["la%d" % t for t in range(ROUNDS)])
+
+
+def rank_program(g, core, T, topo):
+    rank = T.rank_of(core)
+    if rank is None:
+        return
+    n = len(T.cores)
+    nxt, prv = T.cores[(rank + 1) % n], T.cores[(rank - 1) % n]
+    mask = topo.mask(core, nxt)
+    n_out, n_in = len(topo.engines(core, nxt)), len(topo.engines(prv, core))
+    rid, pid = topo.addr(nxt, core)
+    V, S, P, Y = g.vector, g.scalar, g.tensor, g.sync
+    queue = {"v": V, "s": S, "t": P, "g": g, "y": Y}
+    own_sem = {"v": "vec", "s": "sca", "t": "ten", "g": "gps"}
+    count = {"vec": 0, "sca": 0, "ten": 0, "gps": 0, "loc": 0}
+    waited = {}
+    writer, readers = {}, {}
+
+    def W(name, a=0, b=None, step=1):
+        buf, lo, w = PLACE[name]
+        return T[buf][:, lo + a:lo + (w if b is None else b):step]
+
+    def wait(q, tok):
+        sem, val = tok
+        if waited.get((q, sem), 0) < val:
+            queue[q].wait_ge(T.sem[sem], val)
+            waited[(q, sem)] = val
+
+    def order(q, reads, writes, chained=False):
+        need = {}
+        for k in reads:
+            tok = writer[k]
+            need[tok[0]] = max(need.get(tok[0], 0), tok[1])
+        for k in writes:
+            for tok in ([] if chained or k not in writer else [writer[k]]) + [r for r in readers.get(k, []) if r[0] != own_sem.get(q)]:
+                need[tok[0]] = max(need.get(tok[0], 0), tok[1])
+        for sem in need:
+            wait(q, (sem, need[sem]))
+
+    def note(tok, reads, writes):
+        for k in reads:
+            readers.setdefault(k, []).append(tok)
+        for k in writes:
+            writer[k] = tok
+            readers[k] = []
+
+    def do(q, reads, writes, call, chained=False):
+        order(q, reads, writes, chained)
+        sem = own_sem[q]
+        call().then_inc(T.sem[sem], 1)
+        count[sem] += 1
+        note((sem, count[sem]), reads, writes)
+
+    def load(q, buf, out, src, sem, total, key=None):
+        queue[q].dma_start(out, src).then_inc(T.sem[sem], 16)
+        note((sem, total), [], [key or buf])
+
+    def send(out, src, sem, reads):
+        order("g", reads, [])
+        g.remote_dma(out, src, T.sem[sem], T.sem.loc, pid, rid, mask)
+        count["loc"] += n_out
+
+    def tt(out, a, b, op, reads, writes):
+        do("v", reads, writes, lambda: V.tensor_tensor(out, a, b, op))
+
+    def ts(out, a, s1, op0, reads, writes, s2=None, op1=None):
+        if op1 is None:
+            do("v", reads, writes, lambda: V.tensor_scalar(out, a, s1, None, op0))
+        else:
+            do("v", reads, writes, lambda: V.tensor_scalar(out, a, s1, s2, op0, op1))
+
+    def cp(out, a, reads, writes):
+        do("v", reads, writes, lambda: V.tensor_copy(out, a))
+
+    def act(out, a, scale, reads, writes):
+        do("s", reads, writes, lambda: S.activation(out, a, COPY, scale=scale))
+
+    def scan(out, d0, d1, reads, writes, init=0.0, op0=OP.mult, op1=OP.add):
+        do("v", reads, writes, lambda: V.tensor_tensor_scan(out, d0, d1, init, op0, op1))
+
+    def quant(name, tile, reads):
+        do("v", reads, ["q" + name], lambda: V.quantize_mx(T["q" + name][:], T["s" + name][:], tile))
+
+    def fillc(out, value, key):
+        do("v", [], key, lambda: V.memset(out, value))
+
+    def mm(out, a, x, k, reads, writes, start=True, stop=True, col=0):
+        do("t", reads + ["q" + a, "q" + x], writes,
+           lambda: P.matmul_mx(out, T["q" + a][:, col:col + 128], T["s" + a][:, col:col + 128], T["q" + x][:, 0:k], T["s" + x][:, 0:k], start, stop), chained=not start)
+
+    load("y", "x0", T.x0[:], T.x[:], "dx", 16)
+    load("s", "usb", T.usb[:], T.u[:], "du", 16)
+    load("y", "lst0", T.lst0[:], T.p[:], "dp", 16)
+    for r in range(16):
+        load("y", "prow", T.prow[r:128:16, :], T.p[:], "dr", 256)
+    load("y", "qw", T.qw[:].bitcast(dt.uint8), T.wc[:], "dw", 32)
+    load("y", "qw", T.sw[:], T.ws[:], "dw", 32)
+    load("y", "vsb", T.vsb[:], T.v[:], "dv", 16)
+
+    do("g", [], ["ipcol"], lambda: g.iota(T.ipcol[:], [[1, 1]], 0, 1))
+    do("g", [], ["upick"], lambda: g.iota(T.upick[:], [[16, 8]], 0, 0))
+    do("g", [], ["ft16"], lambda: g.iota(T.ft16[:], [[0, 16], [1, 16]], 0, 0, allow_small_or_imprecise_dtypes=True))
+    do("g", [], ["m16"], lambda: g.iota(W("m16"), [[16, 16]], 0, 0))
+    do("g", [], ["mm"], lambda: g.iota(W("mm"), [[1, 16]], 0, 0))
+    fillc(T.one[:], 1.0, ["one"])
+    do("g", ["one"], ["g1"], lambda: g.affine_select(T.g1[:], T.one[:, 0:512], [[-16, 8], [0, 64]], OP.is_ge, 0.0, 0, 1))
+    do("g", ["g1"], ["g2"], lambda: g.affine_select(T.g2[:], T.g1[:], [[16, 8], [0, 64]], OP.is_ge, 0.0, 15, -1))
+    for name, k, slots in CTILES:
+        lo = 16 * min(m for m in slots if m != "b")
+        fillc(T["c" + name][:, 4 * lo:4 * k], 0.0, ["c%s%d" % (name, i) for i in range(4)])
+    cp(T.u16[:], T.upick[:], ["upick"], ["u16"])
+    ts(T.ik[:], T.ipcol[:], 15, OP.bitwise_and, ["ipcol"], ["ik"])
+    cp(T.fkcol[:], T.ik[:], ["ik"], ["fkcol"])
+    ts(T.feqk[:], T.ft16[:], T.fkcol[:, 0:1], OP.is_equal, ["ft16", "fkcol"], ["feqk"])
+    ts(T.fd0a[:], T.ft16[:], 0.0, OP.is_gt, ["ft16"], ["fd0a"])
+    ts(T.d0b[:], T.ft16[:], 0.0, OP.is_gt, ["ft16"], ["d0b"])
+    ts(T.fmsk[:], T.feqk[:], 2 * BIG, OP.mult, ["feqk"], ["fmsk"], -BIG, OP.add)
+    ts(T.fd0r[:], T.fd0a[:], 2 * BIG, OP.mult, ["fd0a"], ["fd0r"], -BIG, OP.add)
+    quant("u", T.usb[:], ["usb"])
+    do("v", ["qu", "u16"], ["qr"], lambda: V.tensor_copy(T.qr[:].bitcast(dt.uint32), T.qu[:].bitcast(dt.uint32).indirect(T.u16[:])))
+    do("s", ["qu", "u16"], ["qrs"], lambda: S.activation(T.sr[:], T.su[:].indirect(T.u16[:]), COPY))
+    quant("x0", T.x0[:], ["x0"])
+    for b in range(4):
+        act(T.h0[:, 512 * b:512 * b + 256], T.x0[:, b:1024:4], 0.5, ["x0"], ["hx0_%d" % b])
+
+    def weights():
+        ts(W("k1"), T.fkcol[:], 1.0, OP.add, ["fkcol"], ["k1"])
+        ts(W("k16"), T.fkcol[:], 16.0, OP.mult, ["fkcol"], ["k16"])
+        ts(W("kap0"), T.fkcol[:], 15.0, OP.is_equal, ["fkcol"], ["kap0"], 1.0 - 1.0 / LIFT, OP.mult)
+        ts(W("kwa"), T.ft16[:], T.fkcol[:, 0:1], OP.not_equal, ["ft16", "fkcol"], ["kwa"])
+        ts(W("kwb"), T.ft16[:], W("k1"), OP.is_equal, ["ft16", "k1"], ["kwb"], LIFT, OP.mult)
+        ts(W("kap"), W("kap0"), 1.0 / LIFT, OP.add, ["kap0"], ["kap"])
+        ts(W("r16"), W("m16"), T.fkcol[:, 0:1], OP.subtract, ["m16", "fkcol"], ["r16"], 15.0 - OFF, OP.add)
+        tt(W("kw"), W("kwa"), W("kwb"), OP.max, ["kwa", "kwb"], ["kw"])
+        ts(W("ii"), W("m16"), T.fkcol[:, 0:1], OP.add, ["m16", "fkcol"], ["ii"])
+        ts(W("perm"), W("mm"), W("k16"), OP.add, ["mm", "k16"], ["perm"])
+
+    def fill(t):
+        fillc(T["w%d" % t][:, 0:256], 256.0, ["wa%d" % t])
+        fillc(T["w%d" % t][:, 256:512], 0.0, ["wb%d" % t])
+        fillc(T["rs%d" % t][:, 0:1], 0.0, ["rs%d_0" % t])
+
+    def landings(t):
+        return T.lst0[:] if t == 0 else W("lst%d" % t)
+
+    def lists(t):
+        ts(W("e2"), W("ii"), -1024.0, OP.mult, ["ii"], ["e2"])
+        tt(W("neg"), W("ii"), landings(t), OP.subtract, ["ii", "lst%d" % t], ["neg"])
+        tt(W("own"), W("e2"), landings(t), OP.add, ["e2", "lst%d" % t], ["own"])
+
+    def packed(t):
+        tt(W("vr%d" % t), W("lr%d" % t), W("irow"), OP.subtract, ["lr%d" % t, "irow"], ["vr%d" % t])
+
+    for t in range(ROUNDS):
+        last = t == ROUNDS - 1
+        L, Ln, x, xn = "lst%d" % t, "lst%d" % (t + 1), "x%d" % t, "x%d" % (t + 1)
+        h, z, w = T["h%d" % t], T["z%d" % t], T["w%d" % t]
+        send(T["ql%d" % t][:].bitcast(dt.uint8), T["q" + x][:].bitcast(dt.uint8), "ca%d" % t, ["q" + x])
+        send(T["sl%d" % t][:], T["s" + x][:], "ca%d" % t, ["q" + x])
+        note(("ca%d" % t, 2 * n_in), [], ["ql%d" % t])
+        if t == 0:
+            do("g", ["one"], ["ee"], lambda: g.affine_select(T.ee[:], T.one[:], [[-1, 520]], OP.is_equal, 0.0, 4, 4))
+            do("g", [], ["irow"], lambda: g.iota(W("irow"), [[1, 256]], 0, 0, allow_small_or_imprecise_dtypes=True))
+            act(T.ibf[:], W("irow"), 1.0, ["irow"], ["ibf"])
+        mm(T.ps[:, 0:256], "r", x, 256, ["qrs"], ["ps"])
+        tt(T.fd1[:], T.ps[:, 0:256], T.fmsk[:], OP.min, ["ps", "fmsk"], ["fd1"])
+        scan(T.ffw[:], T.fd0r[:], T.fd1[:], ["fd0r", "fd1"], ["ffw"], -BIG, OP.min, OP.max)
+        tt(T.ca[:, 0:1024:4], T.ps[:, 0:256], T.ffw[:], OP.is_le, ["ps", "ffw"], ["ca0"])
+        at = 0
+        for ci, (name, k, slots) in enumerate(CTILES):
+            for i, m in enumerate(slots):
+                if m == "b":
+                    continue
+                key = "c%s%d" % (name, i)
+                view = T["c" + name][:, i:64 * m:4]
+                ts(view, T.ps[:, 0:16 * m], T.ffw[:, 16 * m + 15:16 * m + 16], OP.is_lt, ["ps", "ffw"], [key])
+                do("s", [key], ["junk%d" % m, "rs%d_%d" % (t, m)],
+                   lambda: S.activation(T.junk[:, at:at + 16 * m], view, COPY, accum_out=T["rs%d" % t][:, m:m + 1]))
+                at += 16 * m
+            if t == 0 and ci == 0:
+                quant("g", T.g2[:], ["g2"])
+            quant("c" + name, T["c" + name][:], ["c%s%d" % (name, i) for i in range(4)])
+            mm(T.pc[:, 0:k], "g", "c" + name, k, [], ["pc"], start=ci == 0, stop=ci == 3)
+        if t == 0:
+            for b in range(4):
+                do("v", ["ee"], ["qe"], lambda: V.quantize_mx(T.qe[:, 128 * b:128 * b + 128], T.se[:, 128 * b:128 * b + 128], T.ee[:, 4 - b:516 - b]), chained=True)
+        for b in range(4):
+            mm(T["pp%d" % b][:, 0:256], "e", "l%d" % t, 256, [], ["pp%d" % b], col=128 * b)
+            act(h[:, 512 * b + 256:512 * b + 512], T["pp%d" % b][:, 0:256], 0.5, ["pp%d" % b], ["hd%d_%d" % (t, b)])
+        act(T.xh[:], T[x][:], 0.5, ["x0"] if t == 0 else ["%s_%d" % (x, b) for b in range(4)], ["xh"])
+        scan(T.bsum[:], T.d0b[:], T.ca[:, 0:1024:4], ["d0b", "ca0"], ["bsum"])
+        if t == 0:
+            weights()
+            ts(W("lr0"), T.prow[:].indirect(W("perm")), 1024.0, OP.mult, ["prow", "perm"], ["lr0"])
+            fill(0)
+            lists(0)
+            packed(0)
+        tt(W("q1"), W("r16"), T.bsum[:, 15:256:16], OP.subtract, ["r16", "bsum"], ["q1"])
+        scan(W("ex"), W("kw"), T.pc[:, 0:256], ["kw", "pc"], ["ex"])
+        tt(W("q2"), W("q1"), T["rs%d" % t][:], OP.subtract, ["q1"] + ["rs%d_%d" % (t, m) for m in range(16)], ["q2"])
+        ts(W("r1"), W("ex", 15, 256, 16), W("kap"), OP.mult, ["ex", "kap"], ["r1"])
+        tt(W("rho"), W("r1"), W("q2"), OP.add, ["r1", "q2"], ["rho"])
+        cp(W("rho16"), W("rho"), ["rho"], ["rho16"])
+        ts(W("par"), W("rho"), 254, OP.bitwise_and, ["rho"], ["par"])
+        cp(W("pw").indirect(W("rho16")), W("vr%d" % t), ["rho16", "vr%d" % t], ["pw"])
+        ts(W("rx"), W("par"), 2.0, OP.mult, ["par"], ["rx"], 1.0, OP.add)
+        tt(W("sig"), W("rx"), W("rho"), OP.subtract, ["rx", "rho"], ["sig"])
+        cp(W("rx16"), W("sig"), ["sig"], ["rx16"])
+        tt(W("yy"), W("pw").indirect(W("rx16")), T.feqk[:], OP.mult, ["pw", "rx16", "feqk"], ["yy"])
+        scan(W("fy"), T.fd0a[:], W("yy"), ["fd0a", "yy"], ["fy"])
+        tt(W("ss"), W("fy", 15, 256, 16), W("own"), OP.add, ["fy", "own"], ["ss"])
+        ts(W("tt"), W("ss"), FIELD, OP.bitwise_and, ["ss"], ["tt"])
+        ts(W("c2"), W("ss"), 10, OP.arith_shift_right, ["ss"], ["c2"])
+        ts(W("ok"), W("tt"), 0.0, OP.is_equal, ["tt"], ["ok"])
+        tt(W("y"), W("c2"), W("neg"), OP.add, ["c2", "neg"], ["y"])
+        tt(W("zl"), W("y"), W("ok"), OP.mult, ["y", "ok"], ["zl"])
+        tt(W(Ln), landings(t), W("zl"), OP.add, [L, "zl"], [Ln])
+        cp(W("l16"), W(Ln), [Ln], ["l16"])
+        cp(w[:, 0:512].indirect(W("l16")), T.ibf[:], ["l16", "ibf"], ["wa%d" % t, "wb%d" % t])
+        scan(W("sx"), W("kw"), w[:, 256:512], ["kw", "wb%d" % t], ["sx"])
+        ts(T["xs%d" % t][:], W("sx", 15, 256, 16), W("kap"), OP.mult, ["sx", "kap"], ["xs%d" % t], -OFF, OP.add)
+        send(T["la%d" % t][:], T["xs%d" % t][:], "la%d" % t, ["xs%d" % t])
+        note(("la%d" % t, n_in), [], ["la%d" % t])
+        scan(W("so"), W("kw"), w[:, 0:256], ["kw", "wa%d" % t], ["so"])
+        ts(W("tso"), W("so", 15, 256, 16), W("kap"), OP.mult, ["so", "kap"], ["tso"], -OFF, OP.add)
+        ts(W("c1"), W("ss"), 1023, OP.bitwise_and, ["ss"], ["c1"])
+        tt(W("e1"), W("c1"), W("neg"), OP.add, ["c1", "neg"], ["e1"])
+        tt(W("e2"), W("e1"), W("ok"), OP.mult, ["e1", "ok"], ["e2"])
+        tt(W("sig"), W("ii"), W("e2"), OP.subtract, ["ii", "e2"], ["sig"])
+        cp(W("sig16"), W("sig"), ["sig"], ["sig16"])
+        lr, lrn = "lr%d" % t, "lr%d" % (t + 1)
+        act(W(lrn), W(lr).indirect(W("sig16")), 1.0 / 1024.0 if last else 1.0, [lr, "sig16"], [lrn])
+        if last:
+            order("y", [lrn], [])
+            lo = PLACE[lrn][1]
+            Y.dma_start(T.ol[:], T.rows[0:128:16, lo:lo + 256]).then_inc(T.sem.dl, 16)
+        else:
+            lists(t + 1)
+            fill(t + 1)
+            packed(t + 1)
+        if t == 0:
+            quant("v", T.vsb[:], ["vsb"])
+        tt(W("its"), W("tso"), T["la%d" % t][:], OP.add, ["tso", "la%d" % t], ["its"])
+        cp(W("ts16"), W("its"), ["its"], ["ts16"])
+        for b in range(4):
+            tt(z[:, b:1024:4], h[:, 512 * b:512 * b + 512].indirect(W("ts16")), T.xh[:, b:1024:4], OP.add,
+               ["ts16", "xh", "hx%d_%d" % (t, b), "hd%d_%d" % (t, b)], ["z%d_%d" % (t, b)])
+            act(T.zz[:, 256 * b:256 * b + 256], z[:, b:1024:4], 32.0, ["z%d_%d" % (t, b)], ["zz%d" % b])
+        quant("z%d" % t, z[:], ["z%d_%d" % (t, b) for b in range(4)])
+        for b in range(4):
+            mm(T["pp%d" % b][:, 0:256], "w", "z%d" % t, 256, [], ["pp%d" % b], col=128 * b)
+        for b in range(4):
+            ab = T.ab[:, 256 * b:256 * b + 256]
+            tt(ab, T["pp%d" % b][:, 0:256], T.zz[:, 256 * b:256 * b + 256], OP.add, ["pp%d" % b, "zz%d" % b], ["ab%d" % b])
+            out = T[xn][:, b:1024:4]
+            if b < 3:
+                act(out, ab, 0.03125, ["ab%d" % b], ["%s_%d" % (xn, b)])
+            else:
+                ts(out, ab, 0.03125, OP.mult, ["ab%d" % b], ["%s_%d" % (xn, b)])
+        quant(xn, T[xn][:], ["%s_%d" % (xn, b) for b in range(4)])
+        if not last:
+            for b in range(4):
+                act(T["h%d" % (t + 1)][:, 512 * b:512 * b + 256], T.ab[:, 256 * b:256 * b + 256], 0.015625, ["ab%d" % b], ["hx%d_%d" % (t + 1, b)])
+
+    q = "x%d" % ROUNDS
+    order("y", ["q" + q], [])
+    Y.dma_start(T.oc[:], T["q" + q][:].bitcast(dt.uint8)).then_inc(T.sem.dq, 16)
+    for k in range(4):
+        Y.dma_start(T.osc[4 * k:4 * k + 4, :], T["s" + q][32 * k:32 * k + 4, :]).then_inc(T.sem.dq, 16)
+    mm(T.ps[:, 0:256], "v", q, 256, [], ["ps"])
+    act(T.ysb[:], T.ps[:, 0:256], 1.0, ["ps"], ["ysb"])
+    order("s", ["ysb"], [])
+    S.dma_start(T.y[:], T.ysb[:]).then_inc(T.sem.dy, 16)
+    for sem in ("vec", "sca", "ten", "gps", "loc"):
+        wait("g", (sem, count[sem]))
+    for sem, val in (("dx", 16), ("du", 16), ("dp", 16), ("dr", 256), ("dw", 32), ("dv", 16), ("dq", 80), ("dy", 16), ("dl", 16)):
+        wait("g", (sem, val))
+    for t in range(ROUNDS):
+        wait("g", ("ca%d" % t, 2 * n_in))
+        wait("g", ("la%d" % t, n_in))

@@ -1,21 +1,24 @@
 from concourse.mybir import dt, AluOpType, ActivationFunctionType
 
 OP = AluOpType
-COPY = ActivationFunctionType.Copy
+AF = ActivationFunctionType
 ROUNDS = 3
 BIG = 1e29
 LIFT = 4096.0
 OFF = 0.46875
 FIELD = sum(1 << b for b in (8, 9, 18, 19, 20))
+PAIR = 254 + 512
 
 CTILES = [("a", 256, ["b", 15, 14, 13]), ("b", 192, [12, 11, 10, 9]), ("c", 128, [8, 7, 6, 5]), ("d", 128, [4, 3, 2, 1])]
+ON_SCALAR = [15, 12]
 
 PACKS = {
-    "rows": (256, "float32", ["irow", "kwa", "kwb", "kw", "ex", "pw", "yy", "fy", "sx", "so", "vr0", "vr1", "vr2", "lr0", "lr1", "lr2", "lr3"]),
-    "flist": (16, "float32", ["r16", "q1", "q2", "r1", "ok", "y", "zl", "e1", "e2", "own", "neg"]),
-    "ilist": (16, "int32", ["m16", "mm", "ii", "ss", "c2", "tt", "c1", "rho", "par", "rx", "sig", "tso", "its", "lst1", "lst2", "lst3"]),
-    "ulist": (16, "uint16", ["perm", "rho16", "rx16", "l16", "sig16", "ts16"]),
-    "cols": (1, "float32", ["k1", "k16", "kap0", "kap"]),
+    "rows": (256, "float32", ["irow", "irs", "ex", "yy", "fy", "sx", "so", "vr0", "vr1", "vr2", "lr0", "lr1", "lr2", "lr3", "kwa", "kwb"]),
+    "flist": (16, "float32", ["r16", "q1", "q2", "r1", "ok", "ok1", "y", "zl", "e1", "e2", "own", "neg", "lk", "i1k"]),
+    "ilist": (16, "int32", ["m16", "mm", "ii", "ss", "tt", "c1", "rho", "sig", "tso", "its", "lst1", "lst2", "lst3"]),
+    "iwide": (32, "int32", ["pq", "pm"]),
+    "ulist": (16, "uint16", ["perm", "l16", "sig16", "ts16"]),
+    "cols": (1, "float32", ["k2", "k16", "kap0", "kap"]),
 }
 PLACE = {name: (buf, i * w, w) for buf, (w, _, names) in PACKS.items() for i, name in enumerate(names)}
 
@@ -49,18 +52,21 @@ def _scratch():
     for n, k, _ in CTILES:
         sb("bfloat16", 4 * k, "c" + n)
         mx(k, "c" + n)
-    sb("bfloat16", 520, "one", "ee")
-    sb("bfloat16", 512, "g1", "g2", "usb", "vsb")
-    sb("float32", 256, "ft16", "feqk", "fmsk", "fd0r", "fd0a", "fd1", "ffw", "ysb")
+    sb("bfloat16", 520, "ee")
+    sb("bfloat16", 512, "gj", "gg", "usb", "vsb")
+    sb("bfloat16", 128, "dif")
+    sb("float32", 256, "fd1", "ffw", "ysb")
+    sb("float32", 768, "pw")
+    sb("bfloat16", 256, "t16", "eqk", "fmsk", "d0r", "d0b", "kw", "ibf", "bsum")
     sb("int32", 256, "prow")
     sb("int32", 16, "lst0")
-    sb("bfloat16", 256, "ibf", "d0b", "bsum")
-    sb("bfloat16", 1920, "junk")
-    sb("int32", 1, "ipcol", "ik")
-    sb("float32", 1, "fkcol")
+    sb("bfloat16", 1920, "junk", "sgn")
+    sb("int32", 1, "ipcol", "ik", "ig")
+    sb("float32", 1, "fkcol", "fg")
     sb("int32", 8, "upick")
     sb("uint16", 8, "u16")
-    for n in ("ps", "pc", "pp0", "pp1", "pp2", "pp3"):
+    sb("uint16", 32, "pq16")
+    for n in ("ps", "ps2", "pc", "pp0", "pp1", "pp2", "pp3"):
         s[n] = ("psum", [128, 512], "float32")
     return s
 
@@ -121,9 +127,9 @@ def rank_program(g, core, T, topo):
         count[sem] += 1
         note((sem, count[sem]), reads, writes)
 
-    def load(q, buf, out, src, sem, total, key=None):
+    def load(q, buf, out, src, sem, total):
         queue[q].dma_start(out, src).then_inc(T.sem[sem], 16)
-        note((sem, total), [], [key or buf])
+        note((sem, total), [], [buf])
 
     def send(out, src, sem, reads):
         order("g", reads, [])
@@ -142,8 +148,11 @@ def rank_program(g, core, T, topo):
     def cp(out, a, reads, writes):
         do("v", reads, writes, lambda: V.tensor_copy(out, a))
 
-    def act(out, a, scale, reads, writes):
-        do("s", reads, writes, lambda: S.activation(out, a, COPY, scale=scale))
+    def act(out, a, scale, reads, writes, func=AF.Copy, bias=0.0):
+        if func == AF.Copy:
+            do("s", reads, writes, lambda: S.activation(out, a, func, scale=scale))
+        else:
+            do("s", reads, writes, lambda: S.activation(out, a, func, bias=bias, scale=scale))
 
     def scan(out, d0, d1, reads, writes, init=0.0, op0=OP.mult, op1=OP.add):
         do("v", reads, writes, lambda: V.tensor_tensor_scan(out, d0, d1, init, op0, op1))
@@ -154,9 +163,12 @@ def rank_program(g, core, T, topo):
     def fillc(out, value, key):
         do("v", [], key, lambda: V.memset(out, value))
 
-    def mm(out, a, x, k, reads, writes, start=True, stop=True, col=0):
+    def iota(out, pattern, cm, key):
+        do("g", [], [key], lambda: g.iota(out, pattern, 0, cm, allow_small_or_imprecise_dtypes=True))
+
+    def mm(out, a, x, k, reads, writes, start=True, stop=True, col=0, first=0):
         do("t", reads + ["q" + a, "q" + x], writes,
-           lambda: P.matmul_mx(out, T["q" + a][:, col:col + 128], T["s" + a][:, col:col + 128], T["q" + x][:, 0:k], T["s" + x][:, 0:k], start, stop), chained=not start)
+           lambda: P.matmul_mx(out, T["q" + a][:, col:col + 128], T["s" + a][:, col:col + 128], T["q" + x][:, first:first + k], T["s" + x][:, first:first + k], start, stop), chained=not start)
 
     load("y", "x0", T.x0[:], T.x[:], "dx", 16)
     load("s", "usb", T.usb[:], T.u[:], "du", 16)
@@ -167,44 +179,6 @@ def rank_program(g, core, T, topo):
     load("y", "qw", T.sw[:], T.ws[:], "dw", 32)
     load("y", "vsb", T.vsb[:], T.v[:], "dv", 16)
 
-    do("g", [], ["ipcol"], lambda: g.iota(T.ipcol[:], [[1, 1]], 0, 1))
-    do("g", [], ["upick"], lambda: g.iota(T.upick[:], [[16, 8]], 0, 0))
-    do("g", [], ["ft16"], lambda: g.iota(T.ft16[:], [[0, 16], [1, 16]], 0, 0, allow_small_or_imprecise_dtypes=True))
-    do("g", [], ["m16"], lambda: g.iota(W("m16"), [[16, 16]], 0, 0))
-    do("g", [], ["mm"], lambda: g.iota(W("mm"), [[1, 16]], 0, 0))
-    fillc(T.one[:], 1.0, ["one"])
-    do("g", ["one"], ["g1"], lambda: g.affine_select(T.g1[:], T.one[:, 0:512], [[-16, 8], [0, 64]], OP.is_ge, 0.0, 0, 1))
-    do("g", ["g1"], ["g2"], lambda: g.affine_select(T.g2[:], T.g1[:], [[16, 8], [0, 64]], OP.is_ge, 0.0, 15, -1))
-    for name, k, slots in CTILES:
-        lo = 16 * min(m for m in slots if m != "b")
-        fillc(T["c" + name][:, 4 * lo:4 * k], 0.0, ["c%s%d" % (name, i) for i in range(4)])
-    cp(T.u16[:], T.upick[:], ["upick"], ["u16"])
-    ts(T.ik[:], T.ipcol[:], 15, OP.bitwise_and, ["ipcol"], ["ik"])
-    cp(T.fkcol[:], T.ik[:], ["ik"], ["fkcol"])
-    ts(T.feqk[:], T.ft16[:], T.fkcol[:, 0:1], OP.is_equal, ["ft16", "fkcol"], ["feqk"])
-    ts(T.fd0a[:], T.ft16[:], 0.0, OP.is_gt, ["ft16"], ["fd0a"])
-    ts(T.d0b[:], T.ft16[:], 0.0, OP.is_gt, ["ft16"], ["d0b"])
-    ts(T.fmsk[:], T.feqk[:], 2 * BIG, OP.mult, ["feqk"], ["fmsk"], -BIG, OP.add)
-    ts(T.fd0r[:], T.fd0a[:], 2 * BIG, OP.mult, ["fd0a"], ["fd0r"], -BIG, OP.add)
-    quant("u", T.usb[:], ["usb"])
-    do("v", ["qu", "u16"], ["qr"], lambda: V.tensor_copy(T.qr[:].bitcast(dt.uint32), T.qu[:].bitcast(dt.uint32).indirect(T.u16[:])))
-    do("s", ["qu", "u16"], ["qrs"], lambda: S.activation(T.sr[:], T.su[:].indirect(T.u16[:]), COPY))
-    quant("x0", T.x0[:], ["x0"])
-    for b in range(4):
-        act(T.h0[:, 512 * b:512 * b + 256], T.x0[:, b:1024:4], 0.5, ["x0"], ["hx0_%d" % b])
-
-    def weights():
-        ts(W("k1"), T.fkcol[:], 1.0, OP.add, ["fkcol"], ["k1"])
-        ts(W("k16"), T.fkcol[:], 16.0, OP.mult, ["fkcol"], ["k16"])
-        ts(W("kap0"), T.fkcol[:], 15.0, OP.is_equal, ["fkcol"], ["kap0"], 1.0 - 1.0 / LIFT, OP.mult)
-        ts(W("kwa"), T.ft16[:], T.fkcol[:, 0:1], OP.not_equal, ["ft16", "fkcol"], ["kwa"])
-        ts(W("kwb"), T.ft16[:], W("k1"), OP.is_equal, ["ft16", "k1"], ["kwb"], LIFT, OP.mult)
-        ts(W("kap"), W("kap0"), 1.0 / LIFT, OP.add, ["kap0"], ["kap"])
-        ts(W("r16"), W("m16"), T.fkcol[:, 0:1], OP.subtract, ["m16", "fkcol"], ["r16"], 15.0 - OFF, OP.add)
-        tt(W("kw"), W("kwa"), W("kwb"), OP.max, ["kwa", "kwb"], ["kw"])
-        ts(W("ii"), W("m16"), T.fkcol[:, 0:1], OP.add, ["m16", "fkcol"], ["ii"])
-        ts(W("perm"), W("mm"), W("k16"), OP.add, ["mm", "k16"], ["perm"])
-
     def fill(t):
         fillc(T["w%d" % t][:, 0:256], 256.0, ["wa%d" % t])
         fillc(T["w%d" % t][:, 256:512], 0.0, ["wb%d" % t])
@@ -214,92 +188,143 @@ def rank_program(g, core, T, topo):
         return T.lst0[:] if t == 0 else W("lst%d" % t)
 
     def lists(t):
-        ts(W("e2"), W("ii"), -1024.0, OP.mult, ["ii"], ["e2"])
+        tt(W("own"), W("i1k"), landings(t), OP.add, ["i1k", "lst%d" % t], ["own"])
+        ts(W("lk"), landings(t), 1024.0, OP.mult, ["lst%d" % t], ["lk"])
         tt(W("neg"), W("ii"), landings(t), OP.subtract, ["ii", "lst%d" % t], ["neg"])
-        tt(W("own"), W("e2"), landings(t), OP.add, ["e2", "lst%d" % t], ["own"])
 
-    def packed(t):
-        tt(W("vr%d" % t), W("lr%d" % t), W("irow"), OP.subtract, ["lr%d" % t, "irow"], ["vr%d" % t])
+    iota(T.ipcol[:], [[1, 1]], 1, "ipcol")
+    iota(T.t16[:], [[0, 16], [1, 16]], 0, "t16")
+    iota(T.upick[:], [[16, 8]], 0, "upick")
+    iota(W("m16"), [[16, 16]], 0, "m16")
+    iota(W("mm"), [[1, 16]], 0, "mm")
+    iota(T.dif[:], [[1, 128]], -1, "dif")
+    iota(T.gj[:], [[1, 8], [0, 64]], 0, "gj")
+    fillc(T.ee[:], 0.0, ["ee"])
+    ts(T.ik[:], T.ipcol[:], 15, OP.bitwise_and, ["ipcol"], ["ik"])
+    ts(T.ig[:], T.ipcol[:], 4, OP.arith_shift_right, ["ipcol"], ["ig"])
+    cp(T.fkcol[:], T.ik[:], ["ik"], ["fkcol"])
+    ts(W("k2"), T.ik[:], 2.0, OP.add, ["ik"], ["k2"])
+    cp(T.fg[:], T.ig[:], ["ig"], ["fg"])
+    ts(T.eqk[:], T.t16[:], T.fkcol[:, 0:1], OP.is_equal, ["t16", "fkcol"], ["eqk"], 1024.0, OP.mult)
+    cp(T.u16[:], T.upick[:], ["upick"], ["u16"])
+    act(T.d0b[:], T.t16[:], 1.0, ["t16"], ["d0b"], AF.Sign)
+    act(T.d0r[:], T.d0b[:], 2 * BIG, ["d0b"], ["d0r"], AF.Identity, -BIG)
+    act(T.fmsk[:], T.eqk[:], 2 * BIG / 1024, ["eqk"], ["fmsk"], AF.Identity, -BIG)
+    act(W("kwa"), T.t16[:], -1.0, ["t16", "k2"], ["kwa"], AF.Relu, W("k2"))
+    act(W("kwb"), W("kwa"), -LIFT, ["kwa"], ["kwb"], AF.Abs, LIFT - 0.5)
+    for name, k, slots in CTILES:
+        lo = 16 * min(m for m in slots if m != "b")
+        fillc(T["c" + name][:, 4 * lo:4 * k], 0.0, ["c%s%d" % (name, i) for i in range(4)])
+    ts(W("k16"), T.fkcol[:], 16.0, OP.mult, ["fkcol"], ["k16"])
+    ts(W("kap0"), T.fkcol[:], 15.0, OP.is_equal, ["fkcol"], ["kap0"], 1.0 - 1.0 / LIFT, OP.mult)
+    ts(W("r16"), W("m16"), T.fkcol[:, 0:1], OP.subtract, ["m16", "fkcol"], ["r16"], 15.0 - OFF, OP.add)
+    ts(W("ii"), W("m16"), T.fkcol[:, 0:1], OP.add, ["m16", "fkcol"], ["ii"])
+    ts(W("perm"), W("mm"), W("k16"), OP.add, ["mm", "k16"], ["perm"])
+    ts(W("kap"), W("kap0"), 1.0 / LIFT, OP.add, ["kap0"], ["kap"])
+    ts(W("i1k"), W("ii"), -1024.0, OP.mult, ["ii"], ["i1k"])
+    ts(T.ee[:, 4:516:4], T.dif[:], 0.0, OP.is_equal, ["dif"], ["ee"])
+    fill(0)
+    quant("u", T.usb[:], ["usb"])
+    do("v", ["qu", "u16"], ["qr"], lambda: V.tensor_copy(T.qr[:].bitcast(dt.uint32), T.qu[:].bitcast(dt.uint32).indirect(T.u16[:])))
+    do("s", ["qu", "u16"], ["qrs"], lambda: S.activation(T.sr[:], T.su[:].indirect(T.u16[:]), AF.Copy))
+    quant("x0", T.x0[:], ["x0"])
+    act(T.kw[:], W("kwb"), -1.0, ["kwb"], ["kw"], AF.Relu, LIFT + 0.5)
+
+    at = {m: 8 * m * (m - 1) for m in range(1, 16)}
+    views = {}
+    for name, k, slots in CTILES:
+        for i, m in enumerate(slots):
+            if m != "b":
+                views[m] = (T["c" + name][:, i:64 * m:4], "c%s%d" % (name, i))
 
     for t in range(ROUNDS):
         last = t == ROUNDS - 1
         L, Ln, x, xn = "lst%d" % t, "lst%d" % (t + 1), "x%d" % t, "x%d" % (t + 1)
-        h, z, w = T["h%d" % t], T["z%d" % t], T["w%d" % t]
+        h, z, w, rs = T["h%d" % t], T["z%d" % t], T["w%d" % t], T["rs%d" % t]
         send(T["ql%d" % t][:].bitcast(dt.uint8), T["q" + x][:].bitcast(dt.uint8), "ca%d" % t, ["q" + x])
         send(T["sl%d" % t][:], T["s" + x][:], "ca%d" % t, ["q" + x])
         note(("ca%d" % t, 2 * n_in), [], ["ql%d" % t])
         if t == 0:
-            do("g", ["one"], ["ee"], lambda: g.affine_select(T.ee[:], T.one[:], [[-1, 520]], OP.is_equal, 0.0, 4, 4))
-            do("g", [], ["irow"], lambda: g.iota(W("irow"), [[1, 256]], 0, 0, allow_small_or_imprecise_dtypes=True))
-            act(T.ibf[:], W("irow"), 1.0, ["irow"], ["ibf"])
+            iota(W("irow"), [[1, 256]], 0, "irow")
+            iota(T.pw[:], [[0, 768]], 0, "pw")
         mm(T.ps[:, 0:256], "r", x, 256, ["qrs"], ["ps"])
-        tt(T.fd1[:], T.ps[:, 0:256], T.fmsk[:], OP.min, ["ps", "fmsk"], ["fd1"])
-        scan(T.ffw[:], T.fd0r[:], T.fd1[:], ["fd0r", "fd1"], ["ffw"], -BIG, OP.min, OP.max)
-        tt(T.ca[:, 0:1024:4], T.ps[:, 0:256], T.ffw[:], OP.is_le, ["ps", "ffw"], ["ca0"])
-        at = 0
-        for ci, (name, k, slots) in enumerate(CTILES):
-            for i, m in enumerate(slots):
-                if m == "b":
-                    continue
-                key = "c%s%d" % (name, i)
-                view = T["c" + name][:, i:64 * m:4]
-                ts(view, T.ps[:, 0:16 * m], T.ffw[:, 16 * m + 15:16 * m + 16], OP.is_lt, ["ps", "ffw"], [key])
-                do("s", [key], ["junk%d" % m, "rs%d_%d" % (t, m)],
-                   lambda: S.activation(T.junk[:, at:at + 16 * m], view, COPY, accum_out=T["rs%d" % t][:, m:m + 1]))
-                at += 16 * m
-            if t == 0 and ci == 0:
-                quant("g", T.g2[:], ["g2"])
-            quant("c" + name, T["c" + name][:], ["c%s%d" % (name, i) for i in range(4)])
-            mm(T.pc[:, 0:k], "g", "c" + name, k, [], ["pc"], start=ci == 0, stop=ci == 3)
+        mm(T.ps2[:, 0:256], "r", x, 256, ["qrs"], ["ps2"])
         if t == 0:
             for b in range(4):
                 do("v", ["ee"], ["qe"], lambda: V.quantize_mx(T.qe[:, 128 * b:128 * b + 128], T.se[:, 128 * b:128 * b + 128], T.ee[:, 4 - b:516 - b]), chained=True)
+        tt(T.fd1[:], T.ps[:, 0:256], T.fmsk[:], OP.min, ["ps", "fmsk"], ["fd1"])
+        scan(T.ffw[:], T.d0r[:], T.fd1[:], ["d0r", "fd1"], ["ffw"], -BIG, OP.min, OP.max)
+        tt(T.ca[:, 0:1024:4], T.ps[:, 0:256], T.ffw[:], OP.is_le, ["ps", "ffw"], ["ca0"])
+
+        def count_row(m, view, key, src, func, reads):
+            do("s", reads, [key, "rs%d_%d" % (t, m)], lambda: S.activation(view, src, func, accum_out=rs[:, m:m + 1]))
+        for m in ON_SCALAR:
+            sg = T.sgn[:, at[m]:at[m] + 16 * m]
+            act(sg, T.ps2[:, 0:16 * m], -1.0, ["ps2", "ffw"], ["sgn%d" % m], AF.Sign, T.ffw[:, 16 * m + 15:16 * m + 16])
+            count_row(m, views[m][0], views[m][1], sg, AF.Relu, ["sgn%d" % m])
+        for ci, (name, k, slots) in enumerate(CTILES):
+            for i, m in enumerate(slots):
+                if m == "b" or m in ON_SCALAR:
+                    continue
+                view, key = views[m]
+                ts(view, T.ps[:, 0:16 * m], T.ffw[:, 16 * m + 15:16 * m + 16], OP.is_lt, ["ps", "ffw"], [key])
+                count_row(m, T.junk[:, at[m]:at[m] + 16 * m], "junk%d" % m, view, AF.Copy, [key])
+            if t == 0 and ci == 0:
+                ts(T.gg[:], T.gj[:], T.fg[:, 0:1], OP.is_equal, ["gj", "fg"], ["gg"])
+                quant("g", T.gg[:], ["gg"])
+            quant("c" + name, T["c" + name][:], ["c%s%d" % (name, i) for i in range(4)])
+            mm(T.pc[:, 0:k], "g", "c" + name, k, [], ["pc"], start=ci == 0, stop=ci == 3)
+        xk = ["x0"] * 4 if t == 0 else ["%s_%d" % (x, b) for b in range(4)]
+        if t == 0:
+            act(W("irs"), W("irow"), 1.0 / 1024.0, ["irow"], ["irs"])
+            act(T.ibf[:], W("irow"), 1.0, ["irow"], ["ibf"])
+        for b in range(4):
+            act(h[:, 512 * b:512 * b + 256], T[x][:, b:1024:4], 0.5, [xk[b]], ["hx%d_%d" % (t, b)])
+        act(T.xh[:], T[x][:], 0.5, xk, ["xh"])
         for b in range(4):
             mm(T["pp%d" % b][:, 0:256], "e", "l%d" % t, 256, [], ["pp%d" % b], col=128 * b)
             act(h[:, 512 * b + 256:512 * b + 512], T["pp%d" % b][:, 0:256], 0.5, ["pp%d" % b], ["hd%d_%d" % (t, b)])
-        act(T.xh[:], T[x][:], 0.5, ["x0"] if t == 0 else ["%s_%d" % (x, b) for b in range(4)], ["xh"])
         scan(T.bsum[:], T.d0b[:], T.ca[:, 0:1024:4], ["d0b", "ca0"], ["bsum"])
-        if t == 0:
-            weights()
-            ts(W("lr0"), T.prow[:].indirect(W("perm")), 1024.0, OP.mult, ["prow", "perm"], ["lr0"])
-            fill(0)
-            lists(0)
-            packed(0)
         tt(W("q1"), W("r16"), T.bsum[:, 15:256:16], OP.subtract, ["r16", "bsum"], ["q1"])
-        scan(W("ex"), W("kw"), T.pc[:, 0:256], ["kw", "pc"], ["ex"])
-        tt(W("q2"), W("q1"), T["rs%d" % t][:], OP.subtract, ["q1"] + ["rs%d_%d" % (t, m) for m in range(16)], ["q2"])
+        if t == 0:
+            lists(0)
+            tt(W("vr0"), T.prow[:].indirect(W("perm")), W("irs"), OP.subtract, ["prow", "perm", "irs"], ["vr0"])
+        scan(W("ex"), T.kw[:], T.pc[:, 0:256], ["kw", "pc"], ["ex"])
+        tt(W("q2"), W("q1"), rs[:], OP.subtract, ["q1"] + ["rs%d_%d" % (t, m) for m in range(16)], ["q2"])
         ts(W("r1"), W("ex", 15, 256, 16), W("kap"), OP.mult, ["ex", "kap"], ["r1"])
         tt(W("rho"), W("r1"), W("q2"), OP.add, ["r1", "q2"], ["rho"])
-        cp(W("rho16"), W("rho"), ["rho"], ["rho16"])
-        ts(W("par"), W("rho"), 254, OP.bitwise_and, ["rho"], ["par"])
-        cp(W("pw").indirect(W("rho16")), W("vr%d" % t), ["rho16", "vr%d" % t], ["pw"])
-        ts(W("rx"), W("par"), 2.0, OP.mult, ["par"], ["rx"], 1.0, OP.add)
-        tt(W("sig"), W("rx"), W("rho"), OP.subtract, ["rx", "rho"], ["sig"])
-        cp(W("rx16"), W("sig"), ["sig"], ["rx16"])
-        tt(W("yy"), W("pw").indirect(W("rx16")), T.feqk[:], OP.mult, ["pw", "rx16", "feqk"], ["yy"])
-        scan(W("fy"), T.fd0a[:], W("yy"), ["fd0a", "yy"], ["fy"])
-        tt(W("ss"), W("fy", 15, 256, 16), W("own"), OP.add, ["fy", "own"], ["ss"])
+        ts(W("pq", 0, 16), W("rho"), 513.0, OP.mult, ["rho"], ["pqa"])
+        ts(W("pq", 16, 32), W("rho"), 513.0, OP.mult, ["rho"], ["pqb"], 512.0, OP.add)
+        ts(W("pm"), W("pq"), PAIR, OP.bitwise_and, ["pqa", "pqb"], ["pm"])
+        cp(T.pq16[:], W("pm"), ["pm"], ["pq16"])
+        cp(T.pw[:].indirect(T.pq16[:, 0:16]), W("vr%d" % t), ["pq16", "vr%d" % t], ["pw"])
+        tt(W("yy"), T.pw[:].indirect(T.pq16[:, 16:32]), T.eqk[:], OP.mult, ["pw", "pq16", "eqk"], ["yy"])
+        scan(W("fy"), T.d0b[:], W("yy"), ["d0b", "yy"], ["fy"])
+        fy = W("fy", 15, 256, 16)
+        tt(W("ss"), fy, W("own"), OP.add, ["fy", "own"], ["ss"])
+        tt(W("y"), fy, W("lk"), OP.subtract, ["fy", "lk"], ["y"])
         ts(W("tt"), W("ss"), FIELD, OP.bitwise_and, ["ss"], ["tt"])
-        ts(W("c2"), W("ss"), 10, OP.arith_shift_right, ["ss"], ["c2"])
-        ts(W("ok"), W("tt"), 0.0, OP.is_equal, ["tt"], ["ok"])
-        tt(W("y"), W("c2"), W("neg"), OP.add, ["c2", "neg"], ["y"])
+        ts(W("ok"), W("tt"), 0.0, OP.is_equal, ["tt"], ["ok"], 1.0 / 1024.0, OP.mult)
         tt(W("zl"), W("y"), W("ok"), OP.mult, ["y", "ok"], ["zl"])
         tt(W(Ln), landings(t), W("zl"), OP.add, [L, "zl"], [Ln])
         cp(W("l16"), W(Ln), [Ln], ["l16"])
         cp(w[:, 0:512].indirect(W("l16")), T.ibf[:], ["l16", "ibf"], ["wa%d" % t, "wb%d" % t])
-        scan(W("sx"), W("kw"), w[:, 256:512], ["kw", "wb%d" % t], ["sx"])
+        scan(W("sx"), T.kw[:], w[:, 256:512], ["kw", "wb%d" % t], ["sx"])
         ts(T["xs%d" % t][:], W("sx", 15, 256, 16), W("kap"), OP.mult, ["sx", "kap"], ["xs%d" % t], -OFF, OP.add)
         send(T["la%d" % t][:], T["xs%d" % t][:], "la%d" % t, ["xs%d" % t])
         note(("la%d" % t, n_in), [], ["la%d" % t])
-        scan(W("so"), W("kw"), w[:, 0:256], ["kw", "wa%d" % t], ["so"])
+        scan(W("so"), T.kw[:], w[:, 0:256], ["kw", "wa%d" % t], ["so"])
         ts(W("tso"), W("so", 15, 256, 16), W("kap"), OP.mult, ["so", "kap"], ["tso"], -OFF, OP.add)
+        if t == 0:
+            cp(W("lr0"), T.prow[:].indirect(W("perm")), ["prow", "perm"], ["lr0"])
         ts(W("c1"), W("ss"), 1023, OP.bitwise_and, ["ss"], ["c1"])
+        ts(W("ok1"), W("tt"), 0.0, OP.is_equal, ["tt"], ["ok1"])
         tt(W("e1"), W("c1"), W("neg"), OP.add, ["c1", "neg"], ["e1"])
-        tt(W("e2"), W("e1"), W("ok"), OP.mult, ["e1", "ok"], ["e2"])
+        tt(W("e2"), W("e1"), W("ok1"), OP.mult, ["e1", "ok1"], ["e2"])
         tt(W("sig"), W("ii"), W("e2"), OP.subtract, ["ii", "e2"], ["sig"])
         cp(W("sig16"), W("sig"), ["sig"], ["sig16"])
         lr, lrn = "lr%d" % t, "lr%d" % (t + 1)
-        act(W(lrn), W(lr).indirect(W("sig16")), 1.0 / 1024.0 if last else 1.0, [lr, "sig16"], [lrn])
+        act(W(lrn), W(lr).indirect(W("sig16")), 1.0, [lr, "sig16"], [lrn])
         if last:
             order("y", [lrn], [])
             lo = PLACE[lrn][1]
@@ -307,7 +332,7 @@ def rank_program(g, core, T, topo):
         else:
             lists(t + 1)
             fill(t + 1)
-            packed(t + 1)
+            tt(W("vr%d" % (t + 1)), W(lrn), W("irs"), OP.subtract, [lrn, "irs"], ["vr%d" % (t + 1)])
         if t == 0:
             quant("v", T.vsb[:], ["vsb"])
         tt(W("its"), W("tso"), T["la%d" % t][:], OP.add, ["tso", "la%d" % t], ["its"])
@@ -328,22 +353,23 @@ def rank_program(g, core, T, topo):
             else:
                 ts(out, ab, 0.03125, OP.mult, ["ab%d" % b], ["%s_%d" % (xn, b)])
         quant(xn, T[xn][:], ["%s_%d" % (xn, b) for b in range(4)])
-        if not last:
-            for b in range(4):
-                act(T["h%d" % (t + 1)][:, 512 * b:512 * b + 256], T.ab[:, 256 * b:256 * b + 256], 0.015625, ["ab%d" % b], ["hx%d_%d" % (t + 1, b)])
 
     q = "x%d" % ROUNDS
     order("y", ["q" + q], [])
     Y.dma_start(T.oc[:], T["q" + q][:].bitcast(dt.uint8)).then_inc(T.sem.dq, 16)
     for k in range(4):
         Y.dma_start(T.osc[4 * k:4 * k + 4, :], T["s" + q][32 * k:32 * k + 4, :]).then_inc(T.sem.dq, 16)
-    mm(T.ps[:, 0:256], "v", q, 256, [], ["ps"])
-    act(T.ysb[:], T.ps[:, 0:256], 1.0, ["ps"], ["ysb"])
-    order("s", ["ysb"], [])
-    S.dma_start(T.y[:], T.ysb[:]).then_inc(T.sem.dy, 16)
+    mm(T.ps[:, 0:128], "v", q, 128, [], ["ps"])
+    mm(T.ps2[:, 0:128], "v", q, 128, [], ["ps2"], first=128)
+    cp(T.ysb[:, 0:128], T.ps[:, 0:128], ["ps"], ["ysba"])
+    act(T.ysb[:, 128:256], T.ps2[:, 0:128], 1.0, ["ps2"], ["ysbb"])
+    order("y", ["ysba"], [])
+    Y.dma_start(T.y[:, 0:128], T.ysb[:, 0:128]).then_inc(T.sem.dq, 16)
+    order("s", ["ysbb"], [])
+    S.dma_start(T.y[:, 128:256], T.ysb[:, 128:256]).then_inc(T.sem.dy, 16)
     for sem in ("vec", "sca", "ten", "gps", "loc"):
         wait("g", (sem, count[sem]))
-    for sem, val in (("dx", 16), ("du", 16), ("dp", 16), ("dr", 256), ("dw", 32), ("dv", 16), ("dq", 80), ("dy", 16), ("dl", 16)):
+    for sem, val in (("dx", 16), ("du", 16), ("dp", 16), ("dr", 256), ("dw", 32), ("dv", 16), ("dq", 96), ("dy", 16), ("dl", 16)):
         wait("g", (sem, val))
     for t in range(ROUNDS):
         wait("g", ("ca%d" % t, 2 * n_in))

from concourse.mybir import dt, AluOpType, ActivationFunctionType

OP = AluOpType
AF = ActivationFunctionType
ROUNDS = 3
BIG = 1e29
LIFT = 4096.0
OFF = 0.46875
FIELD = sum(1 << b for b in (8, 9, 18, 19, 20))
PAIR = 254 + 512

CTILES = [("a", 256, ["b", 15, 14, 13]), ("b", 192, [12, 11, 10, 9]), ("c", 128, [8, 7, 6, 5]), ("d", 128, [4, 3, 2, 1])]
ON_SCALAR = [15, 12]

PACKS = {
    "rows": (256, "float32", ["irow", "irs", "ex", "yy", "fy", "sx", "so", "vr0", "vr1", "vr2", "lr0", "lr1", "lr2", "lr3", "kwa", "kwb"]),
    "flist": (16, "float32", ["r16", "q1", "q2", "r1", "ok", "ok1", "y", "zl", "e1", "e2", "own", "neg", "lk", "i1k"]),
    "ilist": (16, "int32", ["m16", "mm", "ii", "ss", "tt", "c1", "rho", "sig", "tso", "its", "lst1", "lst2", "lst3"]),
    "iwide": (32, "int32", ["pq", "pm"]),
    "ulist": (16, "uint16", ["perm", "l16", "sig16", "ts16"]),
    "cols": (1, "float32", ["k2", "k16", "kap0", "kap"]),
}
PLACE = {name: (buf, i * w, w) for buf, (w, _, names) in PACKS.items() for i, name in enumerate(names)}


def _scratch():
    s = {}

    def sb(d, n, *names):
        for name in names:
            s[name] = ("sbuf", [128, n], d)

    def mx(n, *names):
        for name in names:
            sb("float8_e4m3fn_x4", n, "q" + name)
            sb("uint8", n, "s" + name)
    for buf, (w, d, names) in PACKS.items():
        sb(d, w * len(names), buf)
    for t in range(ROUNDS + 1):
        sb("bfloat16", 1024, "x%d" % t)
        mx(256, "x%d" % t)
    for t in range(ROUNDS):
        mx(256, "l%d" % t, "z%d" % t)
        sb("int32", 16, "la%d" % t, "xs%d" % t)
        sb("bfloat16", 1024, "z%d" % t)
        sb("bfloat16", 512, "w%d" % t)
        sb("float32", 16, "rs%d" % t)
        sb("bfloat16", 2048, "h%d" % t)
    sb("bfloat16", 1024, "zz", "ab", "xh")
    mx(512, "w", "e")
    mx(128, "u", "r", "v", "g")
    for n, k, _ in CTILES:
        sb("bfloat16", 4 * k, "c" + n)
        mx(k, "c" + n)
    sb("bfloat16", 520, "ee")
    sb("bfloat16", 512, "gj", "gg", "usb", "vsb")
    sb("bfloat16", 128, "dif")
    sb("float32", 256, "fd1", "ffw", "ysb")
    sb("float32", 768, "pw")
    sb("bfloat16", 256, "t16", "eqk", "fmsk", "d0r", "d0b", "kw", "ibf", "bsum")
    sb("int32", 256, "prow")
    sb("int32", 16, "lst0")
    sb("bfloat16", 1920, "junk", "sgn")
    sb("int32", 1, "ipcol", "ik", "ig")
    sb("float32", 1, "fkcol", "fg")
    sb("int32", 8, "upick")
    sb("uint16", 8, "u16")
    sb("uint16", 32, "pq16")
    for n in ("ps", "ps2", "pc", "pp0", "pp1", "pp2", "pp3"):
        s[n] = ("psum", [128, 512], "float32")
    return s


SCRATCH = _scratch()
SEMAPHORES = (["vec", "sca", "ten", "gps", "dx", "du", "dp", "dr", "dw", "dv", "dq", "dy", "dl", "loc"]
              + ["ca%d" % t for t in range(ROUNDS)] + ["la%d" % t for t in range(ROUNDS)])


def rank_program(g, core, T, topo):
    rank = T.rank_of(core)
    if rank is None:
        return
    n = len(T.cores)
    nxt, prv = T.cores[(rank + 1) % n], T.cores[(rank - 1) % n]
    mask = topo.mask(core, nxt)
    n_out, n_in = len(topo.engines(core, nxt)), len(topo.engines(prv, core))
    rid, pid = topo.addr(nxt, core)
    V, S, P, Y = g.vector, g.scalar, g.tensor, g.sync
    queue = {"v": V, "s": S, "t": P, "g": g, "y": Y}
    own_sem = {"v": "vec", "s": "sca", "t": "ten", "g": "gps"}
    count = {"vec": 0, "sca": 0, "ten": 0, "gps": 0, "loc": 0}
    waited = {}
    writer, readers = {}, {}

    def W(name, a=0, b=None, step=1):
        buf, lo, w = PLACE[name]
        return T[buf][:, lo + a:lo + (w if b is None else b):step]

    def wait(q, tok):
        sem, val = tok
        if waited.get((q, sem), 0) < val:
            queue[q].wait_ge(T.sem[sem], val)
            waited[(q, sem)] = val

    def order(q, reads, writes, chained=False):
        need = {}
        for k in reads:
            tok = writer[k]
            need[tok[0]] = max(need.get(tok[0], 0), tok[1])
        for k in writes:
            for tok in ([] if chained or k not in writer else [writer[k]]) + [r for r in readers.get(k, []) if r[0] != own_sem.get(q)]:
                need[tok[0]] = max(need.get(tok[0], 0), tok[1])
        for sem in need:
            wait(q, (sem, need[sem]))

    def note(tok, reads, writes):
        for k in reads:
            readers.setdefault(k, []).append(tok)
        for k in writes:
            writer[k] = tok
            readers[k] = []

    def do(q, reads, writes, call, chained=False):
        order(q, reads, writes, chained)
        sem = own_sem[q]
        call().then_inc(T.sem[sem], 1)
        count[sem] += 1
        note((sem, count[sem]), reads, writes)

    def load(q, buf, out, src, sem, total):
        queue[q].dma_start(out, src).then_inc(T.sem[sem], 16)
        note((sem, total), [], [buf])

    def send(out, src, sem, reads):
        order("g", reads, [])
        g.remote_dma(out, src, T.sem[sem], T.sem.loc, pid, rid, mask)
        count["loc"] += n_out

    def tt(out, a, b, op, reads, writes):
        do("v", reads, writes, lambda: V.tensor_tensor(out, a, b, op))

    def ts(out, a, s1, op0, reads, writes, s2=None, op1=None):
        if op1 is None:
            do("v", reads, writes, lambda: V.tensor_scalar(out, a, s1, None, op0))
        else:
            do("v", reads, writes, lambda: V.tensor_scalar(out, a, s1, s2, op0, op1))

    def cp(out, a, reads, writes):
        do("v", reads, writes, lambda: V.tensor_copy(out, a))

    def act(out, a, scale, reads, writes, func=AF.Copy, bias=0.0):
        if func == AF.Copy:
            do("s", reads, writes, lambda: S.activation(out, a, func, scale=scale))
        else:
            do("s", reads, writes, lambda: S.activation(out, a, func, bias=bias, scale=scale))

    def scan(out, d0, d1, reads, writes, init=0.0, op0=OP.mult, op1=OP.add):
        do("v", reads, writes, lambda: V.tensor_tensor_scan(out, d0, d1, init, op0, op1))

    def quant(name, tile, reads):
        do("v", reads, ["q" + name], lambda: V.quantize_mx(T["q" + name][:], T["s" + name][:], tile))

    def fillc(out, value, key):
        do("v", [], key, lambda: V.memset(out, value))

    def iota(out, pattern, cm, key):
        do("g", [], [key], lambda: g.iota(out, pattern, 0, cm, allow_small_or_imprecise_dtypes=True))

    def mm(out, a, x, k, reads, writes, start=True, stop=True, col=0, first=0):
        do("t", reads + ["q" + a, "q" + x], writes,
           lambda: P.matmul_mx(out, T["q" + a][:, col:col + 128], T["s" + a][:, col:col + 128], T["q" + x][:, first:first + k], T["s" + x][:, first:first + k], start, stop), chained=not start)

    load("y", "x0", T.x0[:], T.x[:], "dx", 16)
    load("s", "usb", T.usb[:], T.u[:], "du", 16)
    load("y", "lst0", T.lst0[:], T.p[:], "dp", 16)
    for r in range(16):
        load("y", "prow", T.prow[r:128:16, :], T.p[:], "dr", 256)
    load("y", "qw", T.qw[:].bitcast(dt.uint8), T.wc[:], "dw", 32)
    load("y", "qw", T.sw[:], T.ws[:], "dw", 32)
    load("y", "vsb", T.vsb[:], T.v[:], "dv", 16)

    def fill(t):
        fillc(T["w%d" % t][:, 0:256], 256.0, ["wa%d" % t])
        fillc(T["w%d" % t][:, 256:512], 0.0, ["wb%d" % t])
        fillc(T["rs%d" % t][:, 0:1], 0.0, ["rs%d_0" % t])

    def landings(t):
        return T.lst0[:] if t == 0 else W("lst%d" % t)

    def lists(t):
        tt(W("own"), W("i1k"), landings(t), OP.add, ["i1k", "lst%d" % t], ["own"])
        ts(W("lk"), landings(t), 1024.0, OP.mult, ["lst%d" % t], ["lk"])
        tt(W("neg"), W("ii"), landings(t), OP.subtract, ["ii", "lst%d" % t], ["neg"])

    iota(T.ipcol[:], [[1, 1]], 1, "ipcol")
    iota(T.t16[:], [[0, 16], [1, 16]], 0, "t16")
    iota(T.upick[:], [[16, 8]], 0, "upick")
    iota(W("m16"), [[16, 16]], 0, "m16")
    iota(W("mm"), [[1, 16]], 0, "mm")
    iota(T.dif[:], [[1, 128]], -1, "dif")
    iota(T.gj[:], [[1, 8], [0, 64]], 0, "gj")
    fillc(T.ee[:], 0.0, ["ee"])
    ts(T.ik[:], T.ipcol[:], 15, OP.bitwise_and, ["ipcol"], ["ik"])
    ts(T.ig[:], T.ipcol[:], 4, OP.arith_shift_right, ["ipcol"], ["ig"])
    cp(T.fkcol[:], T.ik[:], ["ik"], ["fkcol"])
    ts(W("k2"), T.ik[:], 2.0, OP.add, ["ik"], ["k2"])
    cp(T.fg[:], T.ig[:], ["ig"], ["fg"])
    ts(T.eqk[:], T.t16[:], T.fkcol[:, 0:1], OP.is_equal, ["t16", "fkcol"], ["eqk"], 1024.0, OP.mult)
    cp(T.u16[:], T.upick[:], ["upick"], ["u16"])
    act(T.d0b[:], T.t16[:], 1.0, ["t16"], ["d0b"], AF.Sign)
    act(T.d0r[:], T.d0b[:], 2 * BIG, ["d0b"], ["d0r"], AF.Identity, -BIG)
    act(T.fmsk[:], T.eqk[:], 2 * BIG / 1024, ["eqk"], ["fmsk"], AF.Identity, -BIG)
    act(W("kwa"), T.t16[:], -1.0, ["t16", "k2"], ["kwa"], AF.Relu, W("k2"))
    act(W("kwb"), W("kwa"), -LIFT, ["kwa"], ["kwb"], AF.Abs, LIFT - 0.5)
    for name, k, slots in CTILES:
        lo = 16 * min(m for m in slots if m != "b")
        fillc(T["c" + name][:, 4 * lo:4 * k], 0.0, ["c%s%d" % (name, i) for i in range(4)])
    ts(W("k16"), T.fkcol[:], 16.0, OP.mult, ["fkcol"], ["k16"])
    ts(W("kap0"), T.fkcol[:], 15.0, OP.is_equal, ["fkcol"], ["kap0"], 1.0 - 1.0 / LIFT, OP.mult)
    ts(W("r16"), W("m16"), T.fkcol[:, 0:1], OP.subtract, ["m16", "fkcol"], ["r16"], 15.0 - OFF, OP.add)
    ts(W("ii"), W("m16"), T.fkcol[:, 0:1], OP.add, ["m16", "fkcol"], ["ii"])
    ts(W("perm"), W("mm"), W("k16"), OP.add, ["mm", "k16"], ["perm"])
    ts(W("kap"), W("kap0"), 1.0 / LIFT, OP.add, ["kap0"], ["kap"])
    ts(W("i1k"), W("ii"), -1024.0, OP.mult, ["ii"], ["i1k"])
    ts(T.ee[:, 4:516:4], T.dif[:], 0.0, OP.is_equal, ["dif"], ["ee"])
    fill(0)
    quant("u", T.usb[:], ["usb"])
    do("v", ["qu", "u16"], ["qr"], lambda: V.tensor_copy(T.qr[:].bitcast(dt.uint32), T.qu[:].bitcast(dt.uint32).indirect(T.u16[:])))
    do("s", ["qu", "u16"], ["qrs"], lambda: S.activation(T.sr[:], T.su[:].indirect(T.u16[:]), AF.Copy))
    quant("x0", T.x0[:], ["x0"])
    act(T.kw[:], W("kwb"), -1.0, ["kwb"], ["kw"], AF.Relu, LIFT + 0.5)

    at = {m: 8 * m * (m - 1) for m in range(1, 16)}
    views = {}
    for name, k, slots in CTILES:
        for i, m in enumerate(slots):
            if m != "b":
                views[m] = (T["c" + name][:, i:64 * m:4], "c%s%d" % (name, i))

    for t in range(ROUNDS):
        last = t == ROUNDS - 1
        L, Ln, x, xn = "lst%d" % t, "lst%d" % (t + 1), "x%d" % t, "x%d" % (t + 1)
        h, z, w, rs = T["h%d" % t], T["z%d" % t], T["w%d" % t], T["rs%d" % t]
        send(T["ql%d" % t][:].bitcast(dt.uint8), T["q" + x][:].bitcast(dt.uint8), "ca%d" % t, ["q" + x])
        send(T["sl%d" % t][:], T["s" + x][:], "ca%d" % t, ["q" + x])
        note(("ca%d" % t, 2 * n_in), [], ["ql%d" % t])
        if t == 0:
            iota(W("irow"), [[1, 256]], 0, "irow")
            iota(T.pw[:], [[0, 768]], 0, "pw")
        mm(T.ps[:, 0:256], "r", x, 256, ["qrs"], ["ps"])
        mm(T.ps2[:, 0:256], "r", x, 256, ["qrs"], ["ps2"])
        if t == 0:
            for b in range(4):
                do("v", ["ee"], ["qe"], lambda: V.quantize_mx(T.qe[:, 128 * b:128 * b + 128], T.se[:, 128 * b:128 * b + 128], T.ee[:, 4 - b:516 - b]), chained=True)
        tt(T.fd1[:], T.ps[:, 0:256], T.fmsk[:], OP.min, ["ps", "fmsk"], ["fd1"])
        scan(T.ffw[:], T.d0r[:], T.fd1[:], ["d0r", "fd1"], ["ffw"], -BIG, OP.min, OP.max)
        tt(T.ca[:, 0:1024:4], T.ps[:, 0:256], T.ffw[:], OP.is_le, ["ps", "ffw"], ["ca0"])

        def count_row(m, view, key, src, func, reads):
            do("s", reads, [key, "rs%d_%d" % (t, m)], lambda: S.activation(view, src, func, accum_out=rs[:, m:m + 1]))
        for m in ON_SCALAR:
            sg = T.sgn[:, at[m]:at[m] + 16 * m]
            act(sg, T.ps2[:, 0:16 * m], -1.0, ["ps2", "ffw"], ["sgn%d" % m], AF.Sign, T.ffw[:, 16 * m + 15:16 * m + 16])
            count_row(m, views[m][0], views[m][1], sg, AF.Relu, ["sgn%d" % m])
        for ci, (name, k, slots) in enumerate(CTILES):
            for i, m in enumerate(slots):
                if m == "b" or m in ON_SCALAR:
                    continue
                view, key = views[m]
                ts(view, T.ps[:, 0:16 * m], T.ffw[:, 16 * m + 15:16 * m + 16], OP.is_lt, ["ps", "ffw"], [key])
                count_row(m, T.junk[:, at[m]:at[m] + 16 * m], "junk%d" % m, view, AF.Copy, [key])
            if t == 0 and ci == 0:
                ts(T.gg[:], T.gj[:], T.fg[:, 0:1], OP.is_equal, ["gj", "fg"], ["gg"])
                quant("g", T.gg[:], ["gg"])
            quant("c" + name, T["c" + name][:], ["c%s%d" % (name, i) for i in range(4)])
            mm(T.pc[:, 0:k], "g", "c" + name, k, [], ["pc"], start=ci == 0, stop=ci == 3)
        xk = ["x0"] * 4 if t == 0 else ["%s_%d" % (x, b) for b in range(4)]
        if t == 0:
            act(W("irs"), W("irow"), 1.0 / 1024.0, ["irow"], ["irs"])
            act(T.ibf[:], W("irow"), 1.0, ["irow"], ["ibf"])
        for b in range(4):
            act(h[:, 512 * b:512 * b + 256], T[x][:, b:1024:4], 0.5, [xk[b]], ["hx%d_%d" % (t, b)])
        act(T.xh[:], T[x][:], 0.5, xk, ["xh"])
        for b in range(4):
            mm(T["pp%d" % b][:, 0:256], "e", "l%d" % t, 256, [], ["pp%d" % b], col=128 * b)
            act(h[:, 512 * b + 256:512 * b + 512], T["pp%d" % b][:, 0:256], 0.5, ["pp%d" % b], ["hd%d_%d" % (t, b)])
        scan(T.bsum[:], T.d0b[:], T.ca[:, 0:1024:4], ["d0b", "ca0"], ["bsum"])
        tt(W("q1"), W("r16"), T.bsum[:, 15:256:16], OP.subtract, ["r16", "bsum"], ["q1"])
        if t == 0:
            lists(0)
            tt(W("vr0"), T.prow[:].indirect(W("perm")), W("irs"), OP.subtract, ["prow", "perm", "irs"], ["vr0"])
        scan(W("ex"), T.kw[:], T.pc[:, 0:256], ["kw", "pc"], ["ex"])
        tt(W("q2"), W("q1"), rs[:], OP.subtract, ["q1"] + ["rs%d_%d" % (t, m) for m in range(16)], ["q2"])
        ts(W("r1"), W("ex", 15, 256, 16), W("kap"), OP.mult, ["ex", "kap"], ["r1"])
        tt(W("rho"), W("r1"), W("q2"), OP.add, ["r1", "q2"], ["rho"])
        ts(W("pq", 0, 16), W("rho"), 513.0, OP.mult, ["rho"], ["pqa"])
        ts(W("pq", 16, 32), W("rho"), 513.0, OP.mult, ["rho"], ["pqb"], 512.0, OP.add)
        ts(W("pm"), W("pq"), PAIR, OP.bitwise_and, ["pqa", "pqb"], ["pm"])
        cp(T.pq16[:], W("pm"), ["pm"], ["pq16"])
        cp(T.pw[:].indirect(T.pq16[:, 0:16]), W("vr%d" % t), ["pq16", "vr%d" % t], ["pw"])
        tt(W("yy"), T.pw[:].indirect(T.pq16[:, 16:32]), T.eqk[:], OP.mult, ["pw", "pq16", "eqk"], ["yy"])
        scan(W("fy"), T.d0b[:], W("yy"), ["d0b", "yy"], ["fy"])
        fy = W("fy", 15, 256, 16)
        tt(W("ss"), fy, W("own"), OP.add, ["fy", "own"], ["ss"])
        tt(W("y"), fy, W("lk"), OP.subtract, ["fy", "lk"], ["y"])
        ts(W("tt"), W("ss"), FIELD, OP.bitwise_and, ["ss"], ["tt"])
        ts(W("ok"), W("tt"), 0.0, OP.is_equal, ["tt"], ["ok"], 1.0 / 1024.0, OP.mult)
        tt(W("zl"), W("y"), W("ok"), OP.mult, ["y", "ok"], ["zl"])
        tt(W(Ln), landings(t), W("zl"), OP.add, [L, "zl"], [Ln])
        cp(W("l16"), W(Ln), [Ln], ["l16"])
        cp(w[:, 0:512].indirect(W("l16")), T.ibf[:], ["l16", "ibf"], ["wa%d" % t, "wb%d" % t])
        scan(W("sx"), T.kw[:], w[:, 256:512], ["kw", "wb%d" % t], ["sx"])
        ts(T["xs%d" % t][:], W("sx", 15, 256, 16), W("kap"), OP.mult, ["sx", "kap"], ["xs%d" % t], -OFF, OP.add)
        send(T["la%d" % t][:], T["xs%d" % t][:], "la%d" % t, ["xs%d" % t])
        note(("la%d" % t, n_in), [], ["la%d" % t])
        scan(W("so"), T.kw[:], w[:, 0:256], ["kw", "wa%d" % t], ["so"])
        ts(W("tso"), W("so", 15, 256, 16), W("kap"), OP.mult, ["so", "kap"], ["tso"], -OFF, OP.add)
        if t == 0:
            cp(W("lr0"), T.prow[:].indirect(W("perm")), ["prow", "perm"], ["lr0"])
        ts(W("c1"), W("ss"), 1023, OP.bitwise_and, ["ss"], ["c1"])
        ts(W("ok1"), W("tt"), 0.0, OP.is_equal, ["tt"], ["ok1"])
        tt(W("e1"), W("c1"), W("neg"), OP.add, ["c1", "neg"], ["e1"])
        tt(W("e2"), W("e1"), W("ok1"), OP.mult, ["e1", "ok1"], ["e2"])
        tt(W("sig"), W("ii"), W("e2"), OP.subtract, ["ii", "e2"], ["sig"])
        cp(W("sig16"), W("sig"), ["sig"], ["sig16"])
        lr, lrn = "lr%d" % t, "lr%d" % (t + 1)
        act(W(lrn), W(lr).indirect(W("sig16")), 1.0, [lr, "sig16"], [lrn])
        if last:
            order("y", [lrn], [])
            lo = PLACE[lrn][1]
            Y.dma_start(T.ol[:], T.rows[0:128:16, lo:lo + 256]).then_inc(T.sem.dl, 16)
        else:
            lists(t + 1)
            fill(t + 1)
            tt(W("vr%d" % (t + 1)), W(lrn), W("irs"), OP.subtract, [lrn, "irs"], ["vr%d" % (t + 1)])
        if t == 0:
            quant("v", T.vsb[:], ["vsb"])
        tt(W("its"), W("tso"), T["la%d" % t][:], OP.add, ["tso", "la%d" % t], ["its"])
        cp(W("ts16"), W("its"), ["its"], ["ts16"])
        for b in range(4):
            tt(z[:, b:1024:4], h[:, 512 * b:512 * b + 512].indirect(W("ts16")), T.xh[:, b:1024:4], OP.add,
               ["ts16", "xh", "hx%d_%d" % (t, b), "hd%d_%d" % (t, b)], ["z%d_%d" % (t, b)])
            act(T.zz[:, 256 * b:256 * b + 256], z[:, b:1024:4], 32.0, ["z%d_%d" % (t, b)], ["zz%d" % b])
        quant("z%d" % t, z[:], ["z%d_%d" % (t, b) for b in range(4)])
        for b in range(4):
            mm(T["pp%d" % b][:, 0:256], "w", "z%d" % t, 256, [], ["pp%d" % b], col=128 * b)
        for b in range(4):
            ab = T.ab[:, 256 * b:256 * b + 256]
            tt(ab, T["pp%d" % b][:, 0:256], T.zz[:, 256 * b:256 * b + 256], OP.add, ["pp%d" % b, "zz%d" % b], ["ab%d" % b])
            out = T[xn][:, b:1024:4]
            if b < 3:
                act(out, ab, 0.03125, ["ab%d" % b], ["%s_%d" % (xn, b)])
            else:
                ts(out, ab, 0.03125, OP.mult, ["ab%d" % b], ["%s_%d" % (xn, b)])
        quant(xn, T[xn][:], ["%s_%d" % (xn, b) for b in range(4)])

    q = "x%d" % ROUNDS
    order("y", ["q" + q], [])
    Y.dma_start(T.oc[:], T["q" + q][:].bitcast(dt.uint8)).then_inc(T.sem.dq, 16)
    for k in range(4):
        Y.dma_start(T.osc[4 * k:4 * k + 4, :], T["s" + q][32 * k:32 * k + 4, :]).then_inc(T.sem.dq, 16)
    mm(T.ps[:, 0:128], "v", q, 128, [], ["ps"])
    mm(T.ps2[:, 0:128], "v", q, 128, [], ["ps2"], first=128)
    cp(T.ysb[:, 0:128], T.ps[:, 0:128], ["ps"], ["ysba"])
    act(T.ysb[:, 128:256], T.ps2[:, 0:128], 1.0, ["ps2"], ["ysbb"])
    order("y", ["ysba"], [])
    Y.dma_start(T.y[:, 0:128], T.ysb[:, 0:128]).then_inc(T.sem.dq, 16)
    order("s", ["ysbb"], [])
    S.dma_start(T.y[:, 128:256], T.ysb[:, 128:256]).then_inc(T.sem.dy, 16)
    for sem in ("vec", "sca", "ten", "gps", "loc"):
        wait("g", (sem, count[sem]))
    for sem, val in (("dx", 16), ("du", 16), ("dp", 16), ("dr", 256), ("dw", 32), ("dv", 16), ("dq", 96), ("dy", 16), ("dl", 16)):
        wait("g", (sem, val))
    for t in range(ROUNDS):
        wait("g", ("ca%d" % t, 2 * n_in))
        wait("g", ("la%d" % t, n_in))
